import numpy as np
import ml_dtypes


def mxq(x, axis, fmt="e4m3"):
    dtype, down = {"e4m3": (ml_dtypes.float8_e4m3fn, 7), "e5m2": (ml_dtypes.float8_e5m2, 14)}[fmt]
    v = np.moveaxis(np.asarray(x, np.float32).astype(ml_dtypes.bfloat16).astype(np.float64), axis, -1)
    blocks = v.reshape(v.shape[:-1] + (-1, 32))
    amax = np.abs(blocks).max(-1, keepdims=True)
    byte = np.maximum(np.where(amax > 0, np.frexp(amax)[1] - 1 + 127, 0) - down, 1)
    scale = np.exp2(byte - 127.0)
    codes = (blocks / scale).astype(np.float32).astype(dtype).astype(np.float64)
    return np.moveaxis((codes * scale).reshape(v.shape), -1, axis)


WIDE = False


def mx_kscale(k):
    if not WIDE:
        return np.ones(k)
    levels = np.array([10, -10, 5, -5, 0])
    if k % 512:
        return np.exp2(np.random.permutation(np.resize(levels, k // 32))).repeat(32)
    a = np.empty((k // 512, 16))
    for p in range(k // 512):
        a[p, :8] = np.random.permutation(np.resize(levels, 8))
        for g in range(8):
            far = levels[np.abs(levels - a[p, g]) >= 10]
            a[p, g + 8] = far[np.random.randint(len(far))]
    return np.exp2(a.ravel()).repeat(32)


BF16 = ml_dtypes.bfloat16


def bf(x):
    return np.asarray(x, np.float32).astype(BF16)


def f64(x):
    return np.asarray(x).astype(np.float64)


NQ, LQ, ND, LD, D, V = 512, 4, 768, 16, 512, 512


def term_weights(x, w, b):
    logits = mxq(x, 2, "e4m3") @ mxq(w, 0, "e4m3")
    pooled = np.max(logits, axis=1)
    return np.log(1.0 + np.maximum(pooled + b, 0.0))


def centre_and_scale(r, g):
    return (r - np.mean(r, axis=0, keepdims=True)) * g


def draw0():
    sq, sd, t = mx_kscale(D), mx_kscale(D), mx_kscale(V)
    return {
        "xq": bf(np.random.standard_normal((NQ, LQ, D)) * sq),
        "xd": bf(np.random.standard_normal((ND, LD, D)) * sd),
        "wq": bf(np.random.standard_normal((D, V)) / np.sqrt(D) / sq[:, None]),
        "wd": bf(np.random.standard_normal((D, V)) / np.sqrt(D) / sd[:, None]),
        "b": bf(-1.0 + 0.5 * np.random.standard_normal(V)),
        "gq": bf((1.0 + 0.1 * np.random.standard_normal(V)) * t),
        "gd": bf((1.0 + 0.1 * np.random.standard_normal(V)) / t),
    }


def core(xq, xd, wq, wd, b, gq, gd):
    rq = term_weights(f64(xq), f64(wq), f64(b))
    rd = term_weights(f64(xd), f64(wd), f64(b))
    cq = centre_and_scale(rq, f64(gq))
    cd = centre_and_scale(rd, f64(gd))
    return mxq(cq, 1, "e4m3") @ mxq(cd, 1, "e4m3").T


def e4m3fn_bytes(y):
    return np.clip(np.asarray(y, np.float64), -448.0, 448.0).astype(np.float32).astype(ml_dtypes.float8_e4m3fn).view(np.uint8)


def e4m3fn_values(b):
    return np.asarray(b, np.uint8).view(ml_dtypes.float8_e4m3fn).astype(np.float64)


def setup_inputs():
    d = draw0()
    x0 = np.asarray(d['xd']).astype(np.float64)
    s = (np.max(np.abs(x0), axis=(0, 1), keepdims=True) / 448.0).astype(np.float32)
    out = {}
    for k, v in d.items():
        if k == 'xd':
            out['xd_bytes'] = e4m3fn_bytes(x0 / s.astype(np.float64))
            out['xd_scale'] = s
        else:
            out[k] = v
    return out


def reference(xq, xd_bytes, xd_scale, wq, wd, b, gq, gd):
    return core(xq, e4m3fn_values(xd_bytes) * xd_scale.astype(np.float64), wq, wd, b, gq, gd)

@@ -1,0 +1,405 @@
+from contextlib import ExitStack
+
+import concourse.mybir as mybir
+from concourse.masks import make_identity
+
+NQ, LQ, ND, LD, D, V = 512, 4, 768, 16, 512, 512
+FLOPS = 2 * (NQ * LQ + ND * LD) * D * V + 2 * NQ * ND * V
+
+F32 = mybir.dt.float32
+BF16 = mybir.dt.bfloat16
+U32 = mybir.dt.uint32
+U8 = mybir.dt.uint8
+FP8 = mybir.dt.float8_e4m3fn
+FP8X4 = mybir.dt.float8_e4m3fn_x4
+ACT = mybir.ActivationFunctionType
+ALU = mybir.AluOpType
+AX = mybir.AxisListType
+
+P = 128
+PACK = 4
+GROUP = 512
+STEP = 1024
+Q_STEPS = NQ * LQ // STEP
+D_STEPS = ND * LD // STEP
+STEPS = Q_STEPS + D_STEPS
+PLANE_TILES = 6
+PLANE_TOK = PLANE_TILES * P
+DOCS_STEP = STEP // LD
+DOC_SPANS = [(0, 256), (256, 512), (512, 640), (640, 768)]
+CHUNK = 256
+N_CHUNKS = ND // CHUNK
+
+
+def tile_efficientspladecentredscores_t_kernel(tc, xq, xd_bytes, xd_scale, wq, wd, b, gq, gd, out):
+    nc = tc.nc
+    with ExitStack() as ctx:
+        keep = ctx.enter_context(tc.tile_pool(name="keep", bufs=1))
+        work = ctx.enter_context(tc.tile_pool(name="work", bufs=1))
+        psum = ctx.enter_context(tc.psum_pool(name="psum", bufs=1))
+        ctx.enter_context(tc.manual_schedule())
+
+        xq_rows = xq.rearrange("(g p) l d -> g p (l d)", p=P)
+        xd_rows = xd_bytes.rearrange("n l d -> (n l) d").rearrange("(s j p) d -> s p j d", p=P, j=STEP // P)
+        rows = {}
+        xbytes = {}
+
+        def load_queries(g):
+            t = work.tile([P, LQ * D], BF16, name="xq_raw", bufs=4, align_bytes=64)
+            nc.sync.dma_start(out=t[:], in_=xq_rows[g])
+            rows[(g // 2, g % 2)] = t
+
+        def load_docs(s):
+            t = work.tile([P, STEP // P * D], U8, name="xd_raw", bufs=D_STEPS, align_bytes=64)
+            nc.sync.dma_start(out=t[:].rearrange("p (j d) -> p j d", d=D), in_=xd_rows[s])
+            xbytes[s + Q_STEPS] = t
+
+        def load_weight(w, name):
+            t = keep.tile([P, PACK, V], BF16, name=name, align_bytes=64)
+            nc.sync.dma_start(out=t[:], in_=w.rearrange("(p j) c -> p j c", j=PACK))
+            return t
+
+        def load_vector(vec, dtype, name):
+            t = keep.tile([P, PACK], dtype, name=name)
+            nc.sync.dma_start(out=t[:], in_=vec.rearrange("(p t) -> p t", t=PACK))
+            return t
+
+        load_queries(0)
+        wq_raw = load_weight(wq, "wq_raw")
+        load_queries(1)
+        load_queries(2)
+        load_docs(0)
+        load_queries(3)
+        wd_raw = load_weight(wd, "wd_raw")
+        k_scale = load_vector(xd_scale.rearrange("a c k -> (a c k)"), F32, "k_scale")
+        for s in range(1, D_STEPS):
+            load_docs(s)
+        b_raw = load_vector(b, BF16, "b_raw")
+        gq_raw = load_vector(gq, BF16, "gq_raw")
+        gd_raw = load_vector(gd, BF16, "gd_raw")
+
+        ident = keep.tile([P, P], F32, name="ident")
+        make_identity(nc, ident[:])
+        warm = keep.tile([P, 1], F32, name="warm")
+        nc.scalar.activation(out=warm[:], in_=ident[:, 0:1], func=ACT.Ln, bias=1.0)
+
+        pooled_q = keep.tile([P, PACK, NQ], F32, name="pooled_q")
+        pooled_d = keep.tile([P, PACK, ND], F32, name="pooled_d")
+        r_q = keep.tile([P, PACK, NQ], F32, name="r_q")
+        r_d = keep.tile([P, PACK, ND], F32, name="r_d")
+
+        def quantize(src, width, name, bufs):
+            codes = work.tile([P, width], U32, name=name + "_codes", bufs=bufs, align_bytes=64)
+            scales = work.tile([P, width], U8, name=name + "_scales", bufs=bufs, align_bytes=64)
+            nc.vector.quantize_mx(out=codes[:].bitcast(FP8X4), scales=scales[:], in_=src)
+            return codes, scales
+
+        def interleave_weight(raw, name):
+            t = keep.tile([P, V * PACK], BF16, name=name, align_bytes=64)
+            nc.vector.tensor_copy(
+                out=t[:].rearrange("p (t m j) -> p t m j", t=PACK, j=PACK),
+                in_=raw[:].rearrange("p j (m t) -> p t m j", t=PACK),
+            )
+            return t
+
+        banks = {}
+        planes = {}
+        packed = {}
+        quant = {}
+        logits = {}
+        weights = {}
+
+        def widen(i, g):
+            if i >= STEPS:
+                return
+            t = work.tile([P, PACK * D], BF16, name="xd_wide", bufs=5, align_bytes=64)
+            nc.scalar.copy(out=t[:], in_=xbytes[i][:, g * PACK * D : (g + 1) * PACK * D].bitcast(FP8))
+            rows[(i, g)] = t
+
+        def turn(i, g):
+            if i >= STEPS:
+                return
+            words = rows[(i, g)][:].bitcast(F32)
+            for h in range(2):
+                if i < Q_STEPS:
+                    slots = [(2 * h + l, u) for l in range(2) for u in range(2)]
+                elif g == 0:
+                    slots = [(j, h) for j in range(4)]
+                else:
+                    slots = [(2 * h + j, u) for u in range(2) for j in range(2)]
+                bank = psum.tile([P, 512], F32, name="turn%d" % (2 * g + h))
+                for n, (j, u) in enumerate(slots):
+                    nc.tensor.transpose(
+                        bank[:, n * P : (n + 1) * P], words[:, 256 * j + u : 256 * (j + 1) : 2], ident[:]
+                    )
+                banks[(i, 2 * g + h)] = bank
+
+        def empty(i, g):
+            if i >= STEPS:
+                return
+            if i < Q_STEPS:
+                t = work.tile([P, GROUP * PACK], BF16, name="q_packed", bufs=4, align_bytes=64)
+                dst = t[:].bitcast(F32).rearrange("p (q h s) -> p q h s", h=2, s=4)
+                for h in range(2):
+                    nc.scalar.copy(out=dst[:, :, h, :], in_=banks[(i, 2 * g + h)][:].rearrange("p (s q) -> p q s", s=4))
+                packed[(i, g)] = t[:]
+                return
+            if g == 0:
+                pl = work.tile([P, PACK, PLANE_TOK], BF16, name="planes", bufs=2, align_bytes=64)
+                planes[i] = pl
+                parts = [(banks[(i, u)][:], u, 0, GROUP) for u in range(2)]
+            else:
+                n = PLANE_TOK - GROUP
+                parts = [(banks[(i, 2)][:, u * n : (u + 1) * n], u, GROUP, PLANE_TOK) for u in range(2)]
+            for src, u, c0, c1 in parts:
+                pairs = src.bitcast(BF16).rearrange("p (n e) -> p n e", e=2)
+                for e in range(2):
+                    t = 2 * u + e
+                    nc.scalar.activation(
+                        out=planes[i][:, t, c0:c1], in_=pairs[:, :, e], func=ACT.Copy, scale=k_scale[:, t : t + 1]
+                    )
+
+        def gpsimd_interleave(dst, src):
+            nc.gpsimd.tensor_scalar(
+                out=dst.rearrange("p (n t) -> p n t", t=PACK),
+                in0=src.rearrange("p t n -> p n t"),
+                scalar1=1.0,
+                scalar2=0.0,
+                op0=ALU.mult,
+                op1=ALU.add,
+            )
+
+        def new_packed():
+            t = work.tile([P, STEP * PACK], BF16, name="d_packed", bufs=1, align_bytes=64)
+            return t
+
+        def interleave(i):
+            t = new_packed()
+            cuts = (0, GROUP, PLANE_TOK) if i == Q_STEPS else (0, PLANE_TOK)
+            for c0, c1 in zip(cuts, cuts[1:]):
+                gpsimd_interleave(t[:, c0 * PACK : c1 * PACK], planes[i][:, :, c0:c1])
+            for g in range(2):
+                packed[(i, g)] = t[:, g * GROUP * PACK : (g + 1) * GROUP * PACK]
+
+        def scale_rest(i):
+            n = STEP - PLANE_TOK
+            nc.vector.tensor_tensor(
+                out=packed[(i, 1)][:, (PLANE_TOK - GROUP) * PACK :].rearrange("p (n u e) -> p n u e", u=2, e=2),
+                in0=banks[(i, 3)][:].bitcast(BF16).rearrange("p (u n e) -> p n u e", u=2, e=2),
+                in1=k_scale[:].rearrange("p (o u e) -> p o u e", o=1, u=2).to_broadcast([P, n, 2, 2]),
+                op=ALU.mult,
+            )
+
+        def quantize_group(i, g):
+            quant[(i, g)] = quantize(packed[(i, g)], GROUP, "x", 4)
+
+        def multiply(i, g, t):
+            w_codes, w_scales = weights["q" if i < Q_STEPS else "d"]
+            codes, scales = quant[(i, g)]
+            acc = psum.tile([P, GROUP], F32, name="acc", bufs=4)
+            nc.tensor.matmul_mx(
+                out=acc[:],
+                lhsT=w_codes[:, t * P : (t + 1) * P].bitcast(FP8X4),
+                lhsT_scale=w_scales[:, t * P : (t + 1) * P],
+                rhs=codes[:].bitcast(FP8X4),
+                rhs_scale=scales[:],
+                start=True,
+                stop=True,
+            )
+            logits[(i, g, t)] = acc
+
+        def pool_max(i, g, t):
+            if i < Q_STEPS:
+                n = GROUP // LQ
+                dst = pooled_q[:, t, (2 * i + g) * n : (2 * i + g + 1) * n]
+            else:
+                n = GROUP // LD
+                c = 2 * (i - Q_STEPS) + g
+                dst = pooled_d[:, t, c * n : (c + 1) * n]
+            nc.vector.tensor_reduce(
+                out=dst, in_=logits[(i, g, t)][:].rearrange("p (n l) -> p n l", n=n), axis=AX.X, op=ALU.max
+            )
+
+        def multiply_group(i, g):
+            for t in range(PACK):
+                multiply(i, g, t)
+
+        def pool_group(i, g):
+            for t in range(PACK):
+                pool_max(i, g, t)
+
+        b32 = keep.tile([P, PACK], F32, name="b32")
+        gq32 = keep.tile([P, PACK], F32, name="gq32")
+        gd32 = keep.tile([P, PACK], F32, name="gd32")
+        gq_mean = keep.tile([P, PACK], F32, name="gq_mean")
+        gd_mean = keep.tile([P, PACK], F32, name="gd_mean")
+        sum_q = keep.tile([P, PACK], F32, name="sum_q")
+        shift_q = keep.tile([P, PACK], F32, name="shift_q")
+        sum_d = keep.tile([P, len(DOC_SPANS), PACK], F32, name="sum_d")
+        shift_d = keep.tile([P, len(DOC_SPANS), PACK], F32, name="shift_d")
+        cq_planes = keep.tile([P, PACK, NQ], BF16, name="cq_planes", align_bytes=64)
+        cd_planes = [keep.tile([P, PACK, CHUNK], BF16, name="cd_planes%d" % c, align_bytes=64) for c in range(N_CHUNKS)]
+
+        def constants():
+            nc.scalar.activation(out=b32[:], in_=b_raw[:], func=ACT.Copy)
+            nc.scalar.activation(out=gq32[:], in_=gq_raw[:], func=ACT.Copy)
+            nc.scalar.activation(out=gd32[:], in_=gd_raw[:], func=ACT.Copy)
+            nc.scalar.activation(out=gq_mean[:], in_=gq_raw[:], func=ACT.Copy, scale=-1.0 / NQ)
+            nc.scalar.activation(out=gd_mean[:], in_=gd_raw[:], func=ACT.Copy, scale=-1.0 / ND)
+
+        def saturate(pooled, r, sums, t, c0, c1):
+            pos = work.tile([P, NQ], F32, name="pos", bufs=2)
+            nc.scalar.activation(out=pos[:, : c1 - c0], in_=pooled[:, t, c0:c1], func=ACT.Relu, bias=b32[:, t : t + 1])
+            nc.scalar.activation(
+                out=r[:, t, c0:c1], in_=pos[:, : c1 - c0], func=ACT.Ln, bias=1.0, accum_out=sums[:, t : t + 1]
+            )
+
+        def query_terms(t):
+            saturate(pooled_q, r_q, sum_q, t, 0, NQ)
+
+        def query_centre(t):
+            nc.scalar.activation(
+                out=shift_q[:, t : t + 1], in_=sum_q[:, t : t + 1], func=ACT.Copy, scale=gq_mean[:, t : t + 1]
+            )
+            nc.scalar.activation(
+                out=cq_planes[:, t, :], in_=r_q[:, t, :], func=ACT.Identity,
+                scale=gq32[:, t : t + 1], bias=shift_q[:, t : t + 1],
+            )
+
+        def doc_terms(n, t):
+            saturate(pooled_d, r_d, sum_d[:, n, :], t, *DOC_SPANS[n])
+            nc.scalar.activation(
+                out=shift_d[:, n, t : t + 1], in_=sum_d[:, n, t : t + 1], func=ACT.Identity,
+                scale=gd_mean[:, t : t + 1], bias=shift_d[:, n - 1, t : t + 1] if n else 0.0,
+            )
+
+        def doc_centre(t):
+            for c in range(N_CHUNKS):
+                nc.scalar.activation(
+                    out=cd_planes[c][:, t, :], in_=r_d[:, t, c * CHUNK : (c + 1) * CHUNK], func=ACT.Identity,
+                    scale=gd32[:, t : t + 1], bias=shift_d[:, len(DOC_SPANS) - 1, t : t + 1],
+                )
+
+        extra = {
+            2: [constants],
+            3: [lambda: query_terms(0)],
+            4: [lambda: query_terms(1)],
+            5: [lambda: query_terms(2)],
+            6: [lambda: query_terms(3)],
+            7: [lambda: query_centre(0), lambda: query_centre(1)],
+            8: [lambda: query_centre(2), lambda: query_centre(3)],
+            9: [lambda: doc_terms(0, 0), lambda: doc_terms(0, 1)],
+            10: [lambda: doc_terms(0, 2), lambda: doc_terms(0, 3)],
+            11: [lambda: [doc_terms(1, t) for t in range(PACK)]],
+            12: [lambda: [doc_terms(2, t) for t in range(PACK)]],
+        }
+
+        wq_packed = interleave_weight(wq_raw, "wq_packed")
+        turn(0, 0)
+        weights["q"] = quantize(wq_packed[:], V, "wq", 1)
+        empty(0, 0)
+        turn(0, 1)
+        quantize_group(0, 0)
+        empty(0, 1)
+        turn(1, 0)
+        multiply_group(0, 0)
+        quantize_group(0, 1)
+        empty(1, 0)
+        widen(2, 0)
+        turn(1, 1)
+        pool_group(0, 0)
+        empty(1, 1)
+        widen(2, 1)
+        turn(2, 0)
+        multiply_group(0, 1)
+        wd_packed = interleave_weight(wd_raw, "wd_packed")
+        empty(2, 0)
+        turn(2, 1)
+        empty(2, 1)
+        widen(3, 0)
+        widen(3, 1)
+
+        last = STEPS - 1
+        for i in range(1, last):
+            quantize_group(i, 0)
+            if i == 1:
+                weights["d"] = quantize(wd_packed[:], V, "wd", 1)
+            quantize_group(i, 1)
+            interleave(i + 1)
+            if i > 1:
+                turn(i + 2, 0)
+            pool_group(i - 1, 1)
+            multiply_group(i, 0)
+            if i == 1:
+                turn(i + 2, 0)
+            empty(i + 2, 0)
+            widen(i + 3, 0)
+            scale_rest(i + 1)
+            turn(i + 2, 1)
+            pool_group(i, 0)
+            if i < last - 1:
+                multiply_group(i, 1)
+            empty(i + 2, 1)
+            widen(i + 3, 1)
+            for job in extra.get(i, []):
+                job()
+
+        order = [(i, g, t) for t in range(PACK) for i, g in ((last - 1, 1), (last, 0), (last, 1))]
+        multiply(*order[0])
+        quantize_group(last, 0)
+        quantize_group(last, 1)
+        cq_packed = new_packed()
+        gpsimd_interleave(cq_packed[:, : NQ * PACK], cq_planes[:])
+        for n in range(1, 4):
+            multiply(*order[n])
+        for n in range(len(order)):
+            pool_max(*order[n])
+            if n + 4 < len(order):
+                multiply(*order[n + 4])
+            if n % 3 == 2:
+                doc_terms(len(DOC_SPANS) - 1, n // 3)
+                doc_centre(n // 3)
+        cq_codes, cq_scales = quantize(cq_packed[:, : NQ * PACK], NQ, "cq", 1)
+
+        out_rows = out.rearrange("(g p) d -> p g d", p=P)
+        cd_packed = {}
+        cd_quant = {}
+
+        def pack_chunk(c):
+            t = work.tile([P, CHUNK * PACK], BF16, name="cd_packed", bufs=N_CHUNKS, align_bytes=64)
+            nc.vector.tensor_copy(
+                out=t[:].rearrange("p (n t) -> p n t", t=PACK), in_=cd_planes[c][:].rearrange("p t n -> p n t")
+            )
+            cd_packed[c] = t
+
+        def scores(c):
+            codes, scales = cd_quant[c]
+            for h in range(2):
+                acc = psum.tile([P, GROUP], F32, name="acc", bufs=4)
+                for g in range(2):
+                    q0 = (2 * h + g) * P
+                    nc.tensor.matmul_mx(
+                        out=acc[:, g * CHUNK : (g + 1) * CHUNK],
+                        lhsT=cq_codes[:, q0 : q0 + P].bitcast(FP8X4),
+                        lhsT_scale=cq_scales[:, q0 : q0 + P],
+                        rhs=codes[:].bitcast(FP8X4),
+                        rhs_scale=scales[:],
+                        start=True,
+                        stop=True,
+                    )
+                res = work.tile([P, 2 * CHUNK], F32, name="res", bufs=2 * N_CHUNKS)
+                if c == N_CHUNKS - 1 and h == 1:
+                    nc.vector.tensor_copy(out=res[:], in_=acc[:])
+                else:
+                    nc.scalar.copy(out=res[:], in_=acc[:])
+                nc.sync.dma_start(
+                    out=out_rows[:, 2 * h : 2 * h + 2, c * CHUNK : (c + 1) * CHUNK],
+                    in_=res[:].rearrange("p (g d) -> p g d", g=2),
+                )
+
+        pack_chunk(0)
+        for c in range(N_CHUNKS):
+            if c + 1 < N_CHUNKS:
+                pack_chunk(c + 1)
+            cd_quant[c] = quantize(cd_packed[c][:], CHUNK, "cd", N_CHUNKS)
+            scores(c)

@@ -23,12 +23,12 @@ STEP = 1024
 Q_STEPS = NQ * LQ // STEP
 D_STEPS = ND * LD // STEP
 STEPS = Q_STEPS + D_STEPS
-PLANE_TILES = 6
-PLANE_TOK = PLANE_TILES * P
-DOCS_STEP = STEP // LD
-DOC_SPANS = [(0, 256), (256, 512), (512, 640), (640, 768)]
-CHUNK = 256
-N_CHUNKS = ND // CHUNK
+PLANE_TOK = 832
+HALF = GROUP // 2
+WORDS = D // 2
+DOC_SPANS = [(0, 512), (512, 704), (704, 768)]
+QUERY_SPANS = [(0, 512)]
+Q_GROUPS = NQ // P
 
 
 def tile_efficientspladecentredscores_t_kernel(tc, xq, xd_bytes, xd_scale, wq, wd, b, gq, gd, out):
@@ -44,39 +44,49 @@ def tile_efficientspladecentredscores_t_kernel(tc, xq, xd_bytes, xd_scale, wq, w
         rows = {}
         xbytes = {}
 
+        def set_rows(i, j0, t):
+            words = t[:].bitcast(F32)
+            for j in range(words.shape[1] // WORDS):
+                rows[(i, j0 + j)] = words[:, j * WORDS : (j + 1) * WORDS]
+
         def load_queries(g):
             t = work.tile([P, LQ * D], BF16, name="xq_raw", bufs=4, align_bytes=64)
             nc.sync.dma_start(out=t[:], in_=xq_rows[g])
-            rows[(g // 2, g % 2)] = t
+            set_rows(D_STEPS + g // 2, PACK * (g % 2), t)
 
         def load_docs(s):
-            t = work.tile([P, STEP // P * D], U8, name="xd_raw", bufs=D_STEPS, align_bytes=64)
+            t = work.tile([P, STEP // P * D], U8, name="xd_raw", bufs=D_STEPS - 1, align_bytes=64)
             nc.sync.dma_start(out=t[:].rearrange("p (j d) -> p j d", d=D), in_=xd_rows[s])
-            xbytes[s + Q_STEPS] = t
+            for g in range(2):
+                xbytes[(s, g)] = t[:, g * PACK * D : (g + 1) * PACK * D]
+
+        def load_doc_tiles(j0, j1):
+            t = keep.tile([P, (j1 - j0) * D], U8, name="xd_first%d" % j0, align_bytes=64)
+            nc.sync.dma_start(out=t[:].rearrange("p (j d) -> p j d", d=D), in_=xd_rows[0][:, j0:j1, :])
+            return t[:]
 
         def load_weight(w, name):
             t = keep.tile([P, PACK, V], BF16, name=name, align_bytes=64)
             nc.sync.dma_start(out=t[:], in_=w.rearrange("(p j) c -> p j c", j=PACK))
             return t
 
-        def load_vector(vec, dtype, name):
+        def load_vector(vec, dtype, name, queue=nc.sync):
             t = keep.tile([P, PACK], dtype, name=name)
-            nc.sync.dma_start(out=t[:], in_=vec.rearrange("(p t) -> p t", t=PACK))
+            queue.dma_start(out=t[:], in_=vec.rearrange("(p t) -> p t", t=PACK))
             return t
 
-        load_queries(0)
-        wq_raw = load_weight(wq, "wq_raw")
-        load_queries(1)
-        load_queries(2)
-        load_docs(0)
-        load_queries(3)
+        k_scale = load_vector(xd_scale.rearrange("a c k -> (a c k)"), F32, "k_scale", nc.scalar)
         wd_raw = load_weight(wd, "wd_raw")
-        k_scale = load_vector(xd_scale.rearrange("a c k -> (a c k)"), F32, "k_scale")
+        first_bytes = [load_doc_tiles(0, 2), load_doc_tiles(2, 4)]
+        xbytes[(0, 1)] = load_doc_tiles(4, 8)
         for s in range(1, D_STEPS):
             load_docs(s)
         b_raw = load_vector(b, BF16, "b_raw")
         gq_raw = load_vector(gq, BF16, "gq_raw")
         gd_raw = load_vector(gd, BF16, "gd_raw")
+        wq_raw = load_weight(wq, "wq_raw")
+        for g in range(Q_GROUPS):
+            load_queries(g)
 
         ident = keep.tile([P, P], F32, name="ident")
         make_identity(nc, ident[:])
@@ -85,22 +95,13 @@ def tile_efficientspladecentredscores_t_kernel(tc, xq, xd_bytes, xd_scale, wq, w
 
         pooled_q = keep.tile([P, PACK, NQ], F32, name="pooled_q")
         pooled_d = keep.tile([P, PACK, ND], F32, name="pooled_d")
-        r_q = keep.tile([P, PACK, NQ], F32, name="r_q")
-        r_d = keep.tile([P, PACK, ND], F32, name="r_d")
+        r_q, r_d = pooled_q, pooled_d
 
         def quantize(src, width, name, bufs):
             codes = work.tile([P, width], U32, name=name + "_codes", bufs=bufs, align_bytes=64)
             scales = work.tile([P, width], U8, name=name + "_scales", bufs=bufs, align_bytes=64)
             nc.vector.quantize_mx(out=codes[:].bitcast(FP8X4), scales=scales[:], in_=src)
             return codes, scales
-
-        def interleave_weight(raw, name):
-            t = keep.tile([P, V * PACK], BF16, name=name, align_bytes=64)
-            nc.vector.tensor_copy(
-                out=t[:].rearrange("p (t m j) -> p t m j", t=PACK, j=PACK),
-                in_=raw[:].rearrange("p j (m t) -> p t m j", t=PACK),
-            )
-            return t
 
         banks = {}
         planes = {}
@@ -109,48 +110,59 @@ def tile_efficientspladecentredscores_t_kernel(tc, xq, xd_bytes, xd_scale, wq, w
         logits = {}
         weights = {}
 
+        def plane_tokens(i):
+            return {0: 0, 1: GROUP, 2: GROUP + HALF}.get(i, PLANE_TOK)
+
         def widen(i, g):
-            if i >= STEPS:
+            if i >= D_STEPS:
                 return
             t = work.tile([P, PACK * D], BF16, name="xd_wide", bufs=5, align_bytes=64)
-            nc.scalar.copy(out=t[:], in_=xbytes[i][:, g * PACK * D : (g + 1) * PACK * D].bitcast(FP8))
-            rows[(i, g)] = t
+            nc.scalar.copy(out=t[:], in_=xbytes[(i, g)].bitcast(FP8))
+            set_rows(i, PACK * g, t)
 
-        def turn(i, g):
-            if i >= STEPS:
-                return
-            words = rows[(i, g)][:].bitcast(F32)
-            for h in range(2):
-                if i < Q_STEPS:
+        def widen_first(h):
+            t = keep.tile([P, 2 * D], BF16, name="xd_wide_first%d" % h, align_bytes=64)
+            nc.scalar.copy(out=t[:], in_=first_bytes[h].bitcast(FP8))
+            set_rows(0, 2 * h, t)
+
+        def turn(i, g, halves=(0, 1)):
+            for h in halves:
+                if i >= D_STEPS:
                     slots = [(2 * h + l, u) for l in range(2) for u in range(2)]
-                elif g == 0:
+                elif plane_tokens(i) >= (g + 1) * GROUP:
                     slots = [(j, h) for j in range(4)]
                 else:
                     slots = [(2 * h + j, u) for u in range(2) for j in range(2)]
                 bank = psum.tile([P, 512], F32, name="turn%d" % (2 * g + h))
                 for n, (j, u) in enumerate(slots):
                     nc.tensor.transpose(
-                        bank[:, n * P : (n + 1) * P], words[:, 256 * j + u : 256 * (j + 1) : 2], ident[:]
+                        bank[:, n * P : (n + 1) * P], rows[(i, PACK * g + j)][:, u::2], ident[:]
                     )
                 banks[(i, 2 * g + h)] = bank
 
         def empty(i, g):
-            if i >= STEPS:
-                return
-            if i < Q_STEPS:
-                t = work.tile([P, GROUP * PACK], BF16, name="q_packed", bufs=4, align_bytes=64)
+            if i >= D_STEPS:
+                if (i, g) == (STEPS - 1, 1):
+                    t = work.tile([P, GROUP * PACK], BF16, name="late_packed", bufs=1, align_bytes=64)
+                else:
+                    t = work.tile([P, GROUP * PACK], BF16, name="q_packed", bufs=3, align_bytes=64)
                 dst = t[:].bitcast(F32).rearrange("p (q h s) -> p q h s", h=2, s=4)
                 for h in range(2):
                     nc.scalar.copy(out=dst[:, :, h, :], in_=banks[(i, 2 * g + h)][:].rearrange("p (s q) -> p q s", s=4))
                 packed[(i, g)] = t[:]
                 return
-            if g == 0:
+            n = plane_tokens(i)
+            parts = []
+            if n >= (g + 1) * GROUP:
                 pl = work.tile([P, PACK, PLANE_TOK], BF16, name="planes", bufs=2, align_bytes=64)
                 planes[i] = pl
                 parts = [(banks[(i, u)][:], u, 0, GROUP) for u in range(2)]
             else:
-                n = PLANE_TOK - GROUP
-                parts = [(banks[(i, 2)][:, u * n : (u + 1) * n], u, GROUP, PLANE_TOK) for u in range(2)]
+                for bank in (2 * g, 2 * g + 1):
+                    k = min(n - bank * HALF, HALF)
+                    if k > 0:
+                        for u in range(2):
+                            parts.append((banks[(i, bank)][:, u * HALF : u * HALF + k], u, bank * HALF, bank * HALF + k))
             for src, u, c0, c1 in parts:
                 pairs = src.bitcast(BF16).rearrange("p (n e) -> p n e", e=2)
                 for e in range(2):
@@ -159,15 +171,8 @@ def tile_efficientspladecentredscores_t_kernel(tc, xq, xd_bytes, xd_scale, wq, w
                         out=planes[i][:, t, c0:c1], in_=pairs[:, :, e], func=ACT.Copy, scale=k_scale[:, t : t + 1]
                     )
 
-        def gpsimd_interleave(dst, src):
-            nc.gpsimd.tensor_scalar(
-                out=dst.rearrange("p (n t) -> p n t", t=PACK),
-                in0=src.rearrange("p t n -> p n t"),
-                scalar1=1.0,
-                scalar2=0.0,
-                op0=ALU.mult,
-                op1=ALU.add,
-            )
+        def gpsimd_copy(dst, src):
+            nc.gpsimd.tensor_scalar(out=dst, in0=src, scalar1=1.0, scalar2=0.0, op0=ALU.mult, op1=ALU.add)
 
         def new_packed():
             t = work.tile([P, STEP * PACK], BF16, name="d_packed", bufs=1, align_bytes=64)
@@ -175,26 +180,40 @@ def tile_efficientspladecentredscores_t_kernel(tc, xq, xd_bytes, xd_scale, wq, w
 
         def interleave(i):
             t = new_packed()
-            cuts = (0, GROUP, PLANE_TOK) if i == Q_STEPS else (0, PLANE_TOK)
-            for c0, c1 in zip(cuts, cuts[1:]):
-                gpsimd_interleave(t[:, c0 * PACK : c1 * PACK], planes[i][:, :, c0:c1])
-            for g in range(2):
-                packed[(i, g)] = t[:, g * GROUP * PACK : (g + 1) * GROUP * PACK]
-
-        def scale_rest(i):
-            n = STEP - PLANE_TOK
-            nc.vector.tensor_tensor(
-                out=packed[(i, 1)][:, (PLANE_TOK - GROUP) * PACK :].rearrange("p (n u e) -> p n u e", u=2, e=2),
-                in0=banks[(i, 3)][:].bitcast(BF16).rearrange("p (u n e) -> p n u e", u=2, e=2),
-                in1=k_scale[:].rearrange("p (o u e) -> p o u e", o=1, u=2).to_broadcast([P, n, 2, 2]),
-                op=ALU.mult,
+            n = plane_tokens(i)
+            gpsimd_copy(
+                t[:, : n * PACK].rearrange("p (n t) -> p n t", t=PACK), planes[i][:, :, :n].rearrange("p t n -> p n t")
             )
+            packed[i] = t[:]
+
+        def scale_rest(i, g):
+            for bank in (2 * g, 2 * g + 1):
+                k = max(plane_tokens(i) - bank * HALF, 0)
+                if k < HALF:
+                    dst = packed[i][:, (bank * HALF + k) * PACK : (bank + 1) * HALF * PACK]
+                    nc.vector.tensor_tensor(
+                        out=dst.rearrange("p (n u e) -> p n u e", u=2, e=2),
+                        in0=banks[(i, bank)][:].bitcast(BF16).rearrange("p (u n e) -> p n u e", u=2, e=2)[:, k:, :, :],
+                        in1=k_scale[:].rearrange("p (o u e) -> p o u e", o=1, u=2).to_broadcast([P, HALF - k, 2, 2]),
+                        op=ALU.mult,
+                    )
 
         def quantize_group(i, g):
             quant[(i, g)] = quantize(packed[(i, g)], GROUP, "x", 4)
 
+        def quantize_step(i):
+            codes, scales = quantize(packed[i], STEP, "d", 3)
+            for g in range(2):
+                quant[(i, g)] = (codes[:, g * GROUP : (g + 1) * GROUP], scales[:, g * GROUP : (g + 1) * GROUP])
+
+        def weight_views(dst, raw):
+            return (
+                dst.rearrange("p (t m j) -> p t m j", t=PACK, j=PACK),
+                raw[:].rearrange("p j (m t) -> p t m j", t=PACK),
+            )
+
         def multiply(i, g, t):
-            w_codes, w_scales = weights["q" if i < Q_STEPS else "d"]
+            w_codes, w_scales = weights["q" if i >= D_STEPS else "d"]
             codes, scales = quant[(i, g)]
             acc = psum.tile([P, GROUP], F32, name="acc", bufs=4)
             nc.tensor.matmul_mx(
@@ -209,12 +228,13 @@ def tile_efficientspladecentredscores_t_kernel(tc, xq, xd_bytes, xd_scale, wq, w
             logits[(i, g, t)] = acc
 
         def pool_max(i, g, t):
-            if i < Q_STEPS:
+            if i >= D_STEPS:
                 n = GROUP // LQ
-                dst = pooled_q[:, t, (2 * i + g) * n : (2 * i + g + 1) * n]
+                c = 2 * (i - D_STEPS) + g
+                dst = pooled_q[:, t, c * n : (c + 1) * n]
             else:
                 n = GROUP // LD
-                c = 2 * (i - Q_STEPS) + g
+                c = 2 * i + g
                 dst = pooled_d[:, t, c * n : (c + 1) * n]
             nc.vector.tensor_reduce(
                 out=dst, in_=logits[(i, g, t)][:].rearrange("p (n l) -> p n l", n=n), axis=AX.X, op=ALU.max
@@ -233,12 +253,13 @@ def tile_efficientspladecentredscores_t_kernel(tc, xq, xd_bytes, xd_scale, wq, w
         gd32 = keep.tile([P, PACK], F32, name="gd32")
         gq_mean = keep.tile([P, PACK], F32, name="gq_mean")
         gd_mean = keep.tile([P, PACK], F32, name="gd_mean")
-        sum_q = keep.tile([P, PACK], F32, name="sum_q")
-        shift_q = keep.tile([P, PACK], F32, name="shift_q")
+        sum_q = keep.tile([P, len(QUERY_SPANS), PACK], F32, name="sum_q")
+        shift_q = keep.tile([P, len(QUERY_SPANS), PACK], F32, name="shift_q")
         sum_d = keep.tile([P, len(DOC_SPANS), PACK], F32, name="sum_d")
         shift_d = keep.tile([P, len(DOC_SPANS), PACK], F32, name="shift_d")
-        cq_planes = keep.tile([P, PACK, NQ], BF16, name="cq_planes", align_bytes=64)
-        cd_planes = [keep.tile([P, PACK, CHUNK], BF16, name="cd_planes%d" % c, align_bytes=64) for c in range(N_CHUNKS)]
+        cd_planes = keep.tile([P, PACK, ND], BF16, name="cd_planes", align_bytes=64)
+        cq_planes = keep.tile([P, NQ * PACK], BF16, name="cq_planes", align_bytes=64)
+        cq_view = cq_planes[:].rearrange("p (g t n) -> p g t n", t=PACK, n=P)
 
         def constants():
             nc.scalar.activation(out=b32[:], in_=b_raw[:], func=ACT.Copy)
@@ -247,159 +268,208 @@ def tile_efficientspladecentredscores_t_kernel(tc, xq, xd_bytes, xd_scale, wq, w
             nc.scalar.activation(out=gq_mean[:], in_=gq_raw[:], func=ACT.Copy, scale=-1.0 / NQ)
             nc.scalar.activation(out=gd_mean[:], in_=gd_raw[:], func=ACT.Copy, scale=-1.0 / ND)
 
-        def saturate(pooled, r, sums, t, c0, c1):
-            pos = work.tile([P, NQ], F32, name="pos", bufs=2)
-            nc.scalar.activation(out=pos[:, : c1 - c0], in_=pooled[:, t, c0:c1], func=ACT.Relu, bias=b32[:, t : t + 1])
+        positive = {}
+        side = {
+            "q": (pooled_q, r_q, sum_q, shift_q, gq_mean, QUERY_SPANS),
+            "d": (pooled_d, r_d, sum_d, shift_d, gd_mean, DOC_SPANS),
+        }
+
+        def span(which, n, t):
+            return side[which][5][n]
+
+        def clamp(which, n, t):
+            c0, c1 = span(which, n, t)
+            pos = work.tile([P, GROUP], F32, name="pos", bufs=4)
             nc.scalar.activation(
-                out=r[:, t, c0:c1], in_=pos[:, : c1 - c0], func=ACT.Ln, bias=1.0, accum_out=sums[:, t : t + 1]
+                out=pos[:, : c1 - c0], in_=side[which][0][:, t, c0:c1], func=ACT.Relu, bias=b32[:, t : t + 1]
+            )
+            positive[t] = pos[:, : c1 - c0]
+
+        def log1p(which, n, t):
+            c0, c1 = span(which, n, t)
+            nc.scalar.activation(
+                out=side[which][1][:, t, c0:c1], in_=positive[t], func=ACT.Ln, bias=1.0,
+                accum_out=side[which][2][:, n, t : t + 1],
             )
 
-        def query_terms(t):
-            saturate(pooled_q, r_q, sum_q, t, 0, NQ)
-
-        def query_centre(t):
+        def shift(which, n, t):
+            sums, shifts, gain = side[which][2:5]
             nc.scalar.activation(
-                out=shift_q[:, t : t + 1], in_=sum_q[:, t : t + 1], func=ACT.Copy, scale=gq_mean[:, t : t + 1]
-            )
-            nc.scalar.activation(
-                out=cq_planes[:, t, :], in_=r_q[:, t, :], func=ACT.Identity,
-                scale=gq32[:, t : t + 1], bias=shift_q[:, t : t + 1],
-            )
-
-        def doc_terms(n, t):
-            saturate(pooled_d, r_d, sum_d[:, n, :], t, *DOC_SPANS[n])
-            nc.scalar.activation(
-                out=shift_d[:, n, t : t + 1], in_=sum_d[:, n, t : t + 1], func=ACT.Identity,
-                scale=gd_mean[:, t : t + 1], bias=shift_d[:, n - 1, t : t + 1] if n else 0.0,
+                out=shifts[:, n, t : t + 1], in_=sums[:, n, t : t + 1], func=ACT.Identity,
+                scale=gain[:, t : t + 1], bias=shifts[:, n - 1, t : t + 1] if span(which, n, t)[0] else 0.0,
             )
 
         def doc_centre(t):
-            for c in range(N_CHUNKS):
+            nc.scalar.activation(
+                out=cd_planes[:, t, :], in_=r_d[:, t, :], func=ACT.Identity,
+                scale=gd32[:, t : t + 1], bias=shift_d[:, len(DOC_SPANS) - 1, t : t + 1],
+            )
+
+        def query_centre(t):
+            gain, offset = gq32[:, t : t + 1], shift_q[:, len(QUERY_SPANS) - 1, t : t + 1]
+            if t < PACK - 1:
+                nc.gpsimd.tensor_scalar(
+                    out=cq_view[:, :, t, :], in0=r_q[:, t, :].rearrange("p (g n) -> p g n", n=P),
+                    scalar1=gain, scalar2=offset, op0=ALU.mult, op1=ALU.add,
+                )
+                return
+            for g in range(Q_GROUPS):
                 nc.scalar.activation(
-                    out=cd_planes[c][:, t, :], in_=r_d[:, t, c * CHUNK : (c + 1) * CHUNK], func=ACT.Identity,
-                    scale=gd32[:, t : t + 1], bias=shift_d[:, len(DOC_SPANS) - 1, t : t + 1],
+                    out=cq_view[:, g, t, :], in_=r_q[:, t, g * P : (g + 1) * P], func=ACT.Identity,
+                    scale=gain, bias=offset,
                 )
 
-        extra = {
-            2: [constants],
-            3: [lambda: query_terms(0)],
-            4: [lambda: query_terms(1)],
-            5: [lambda: query_terms(2)],
-            6: [lambda: query_terms(3)],
-            7: [lambda: query_centre(0), lambda: query_centre(1)],
-            8: [lambda: query_centre(2), lambda: query_centre(3)],
-            9: [lambda: doc_terms(0, 0), lambda: doc_terms(0, 1)],
-            10: [lambda: doc_terms(0, 2), lambda: doc_terms(0, 3)],
-            11: [lambda: [doc_terms(1, t) for t in range(PACK)]],
-            12: [lambda: [doc_terms(2, t) for t in range(PACK)]],
-        }
+        def each_t(job, *args):
+            for t in range(PACK):
+                job(*args, t)
 
-        wq_packed = interleave_weight(wq_raw, "wq_packed")
-        turn(0, 0)
-        weights["q"] = quantize(wq_packed[:], V, "wq", 1)
-        empty(0, 0)
+        last_doc = D_STEPS - 1
+
+        def extra(i, half):
+            if i == last_doc - 3 and half == 1:
+                constants()
+            if i in (last_doc - 2, last_doc - 1):
+                for t in range(2):
+                    (clamp, log1p)[half]("d", 0, 2 * (i - last_doc + 2) + t)
+            if i == last_doc and half == 0:
+                each_t(clamp, "d", 1)
+                each_t(shift, "d", 0)
+                each_t(log1p, "d", 1)
+            if i == last_doc and half == 1:
+                each_t(shift, "d", 1)
+
+        widen_first(0)
+        wd_packed = keep.tile([P, V * PACK], BF16, name="wd_packed", align_bytes=64)
+        dst, src = weight_views(wd_packed[:], wd_raw)
+        nc.vector.tensor_copy(out=dst, in_=src)
+        turn(0, 0, (0,))
+        widen_first(1)
+        turn(0, 0, (1,))
+        weights["d"] = quantize(wd_packed[:], V, "wd", 1)
+        widen(0, 1)
         turn(0, 1)
+        widen(1, 0)
+        widen(1, 1)
+        first = new_packed()
+        packed[0] = first[:]
+        for g in range(2):
+            packed[(0, g)] = first[:, g * GROUP * PACK : (g + 1) * GROUP * PACK]
+        scale_rest(0, 0)
         quantize_group(0, 0)
-        empty(0, 1)
         turn(1, 0)
         multiply_group(0, 0)
-        quantize_group(0, 1)
         empty(1, 0)
-        widen(2, 0)
+        scale_rest(0, 1)
         turn(1, 1)
-        pool_group(0, 0)
-        empty(1, 1)
+        widen(2, 0)
         widen(2, 1)
+        quantize_group(0, 1)
+        interleave(1)
         turn(2, 0)
+        pool_group(0, 0)
         multiply_group(0, 1)
-        wd_packed = interleave_weight(wd_raw, "wd_packed")
         empty(2, 0)
+        widen(3, 0)
+        scale_rest(1, 1)
         turn(2, 1)
         empty(2, 1)
-        widen(3, 0)
         widen(3, 1)
 
-        last = STEPS - 1
-        for i in range(1, last):
-            quantize_group(i, 0)
-            if i == 1:
-                weights["d"] = quantize(wd_packed[:], V, "wd", 1)
-            quantize_group(i, 1)
-            interleave(i + 1)
-            if i > 1:
-                turn(i + 2, 0)
+        for i in range(1, D_STEPS):
+            quantize_step(i)
+            if i < last_doc:
+                interleave(i + 1)
+            else:
+                wq_packed = new_packed()
+                gpsimd_copy(*weight_views(wq_packed[:, : V * PACK], wq_raw))
+            turn(i + 2, 0)
             pool_group(i - 1, 1)
             multiply_group(i, 0)
-            if i == 1:
-                turn(i + 2, 0)
             empty(i + 2, 0)
+            extra(i, 0)
             widen(i + 3, 0)
-            scale_rest(i + 1)
+            if i < last_doc:
+                scale_rest(i + 1, 1)
             turn(i + 2, 1)
             pool_group(i, 0)
-            if i < last - 1:
-                multiply_group(i, 1)
+            multiply_group(i, 1)
             empty(i + 2, 1)
+            extra(i, 1)
             widen(i + 3, 1)
-            for job in extra.get(i, []):
-                job()
+        pool_group(last_doc, 1)
+        for job in (clamp, log1p, shift):
+            each_t(job, "d", len(DOC_SPANS) - 1)
+        each_t(doc_centre)
 
-        order = [(i, g, t) for t in range(PACK) for i, g in ((last - 1, 1), (last, 0), (last, 1))]
-        multiply(*order[0])
-        quantize_group(last, 0)
-        quantize_group(last, 1)
-        cq_packed = new_packed()
-        gpsimd_interleave(cq_packed[:, : NQ * PACK], cq_planes[:])
-        for n in range(1, 4):
-            multiply(*order[n])
-        for n in range(len(order)):
-            pool_max(*order[n])
+        weights["q"] = quantize(wq_packed[:, : V * PACK], V, "wq", 1)
+        q_groups = [(i, g) for i in range(D_STEPS, STEPS) for g in range(2)]
+        order = [(i, g, t) for t in range(PACK) for i, g in q_groups]
+        for i, g in q_groups:
+            quantize_group(i, g)
+            multiply(i, g, 0)
+        cd_packed = work.tile([P, ND * PACK], BF16, name="late_packed", bufs=1, align_bytes=64)
+        gpsimd_copy(cd_packed[:].rearrange("p (n t) -> p n t", t=PACK), cd_planes[:].rearrange("p t n -> p n t"))
+        for n, (i, g, t) in enumerate(order):
+            pool_max(i, g, t)
             if n + 4 < len(order):
                 multiply(*order[n + 4])
-            if n % 3 == 2:
-                doc_terms(len(DOC_SPANS) - 1, n // 3)
-                doc_centre(n // 3)
-        cq_codes, cq_scales = quantize(cq_packed[:, : NQ * PACK], NQ, "cq", 1)
+            if n % 4 == 3:
+                for job in (clamp, log1p, shift):
+                    job("q", 0, t)
+                query_centre(t)
+        cd_quant = [
+            quantize(cd_packed[:, c0 * PACK : c1 * PACK], c1 - c0, "cd%d" % c0, 1) for c0, c1 in ((0, GROUP), (GROUP, ND))
+        ]
 
-        out_rows = out.rearrange("(g p) d -> p g d", p=P)
-        cd_packed = {}
-        cd_quant = {}
+        cq_packed = {}
+        score_banks = {}
 
-        def pack_chunk(c):
-            t = work.tile([P, CHUNK * PACK], BF16, name="cd_packed", bufs=N_CHUNKS, align_bytes=64)
+        def pack_queries(g):
+            t = work.tile([P, P * PACK], BF16, name="cq_packed", bufs=Q_GROUPS, align_bytes=64)
             nc.vector.tensor_copy(
-                out=t[:].rearrange("p (n t) -> p n t", t=PACK), in_=cd_planes[c][:].rearrange("p t n -> p n t")
+                out=t[:].rearrange("p (n t) -> p n t", t=PACK), in_=cq_view[:, g, :, :].rearrange("p t n -> p n t")
             )
-            cd_packed[c] = t
+            cq_packed[g] = t
 
-        def scores(c):
-            codes, scales = cd_quant[c]
-            for h in range(2):
-                acc = psum.tile([P, GROUP], F32, name="acc", bufs=4)
-                for g in range(2):
-                    q0 = (2 * h + g) * P
-                    nc.tensor.matmul_mx(
-                        out=acc[:, g * CHUNK : (g + 1) * CHUNK],
-                        lhsT=cq_codes[:, q0 : q0 + P].bitcast(FP8X4),
-                        lhsT_scale=cq_scales[:, q0 : q0 + P],
-                        rhs=codes[:].bitcast(FP8X4),
-                        rhs_scale=scales[:],
-                        start=True,
-                        stop=True,
-                    )
-                res = work.tile([P, 2 * CHUNK], F32, name="res", bufs=2 * N_CHUNKS)
-                if c == N_CHUNKS - 1 and h == 1:
-                    nc.vector.tensor_copy(out=res[:], in_=acc[:])
-                else:
-                    nc.scalar.copy(out=res[:], in_=acc[:])
-                nc.sync.dma_start(
-                    out=out_rows[:, 2 * h : 2 * h + 2, c * CHUNK : (c + 1) * CHUNK],
-                    in_=res[:].rearrange("p (g d) -> p g d", g=2),
+        def scores(g):
+            codes, scales = quantize(cq_packed[g][:], P, "cq", Q_GROUPS)
+            wide = psum.tile([P, GROUP], F32, name="acc", bufs=4)
+            narrow = psum.tile([P, GROUP], F32, name="turn%d" % g)
+            score_banks[g] = (wide[:], narrow[:, : ND - GROUP])
+            for part in (1, 0):
+                d_codes, d_scales = cd_quant[part]
+                nc.tensor.matmul_mx(
+                    out=score_banks[g][part],
+                    lhsT=codes[:].bitcast(FP8X4),
+                    lhsT_scale=scales[:],
+                    rhs=d_codes[:].bitcast(FP8X4),
+                    rhs_scale=d_scales[:],
+                    start=True,
+                    stop=True,
                 )
 
-        pack_chunk(0)
-        for c in range(N_CHUNKS):
-            if c + 1 < N_CHUNKS:
-                pack_chunk(c + 1)
-            cd_quant[c] = quantize(cd_packed[c][:], CHUNK, "cd", N_CHUNKS)
-            scores(c)
+        def store(g, copies):
+            res = work.tile([P, ND], F32, name="res", bufs=Q_GROUPS)
+            rows_out = out[g * P : (g + 1) * P, :]
+            copies[1](out=res[:, GROUP:], in_=score_banks[g][1])
+            if g == 0:
+                nc.sync.dma_start(out=rows_out[:, GROUP:], in_=res[:, GROUP:])
+            copies[0](out=res[:, :GROUP], in_=score_banks[g][0])
+            if g == 0:
+                nc.sync.dma_start(out=rows_out[:, :GROUP], in_=res[:, :GROUP])
+            else:
+                nc.sync.dma_start(out=rows_out, in_=res[:])
+
+        on_scalar, on_vector = nc.scalar.copy, nc.vector.tensor_copy
+        pack_queries(0)
+        pack_queries(1)
+        scores(0)
+        pack_queries(2)
+        scores(1)
+        pack_queries(3)
+        scores(2)
+        scores(3)
+        store(0, (on_scalar, on_scalar))
+        store(1, (on_scalar, on_vector))
+        store(2, (on_scalar, on_vector))
+        store(3, (on_vector, on_scalar))

@@ -27,7 +27,7 @@ PLANE_TOK = 832
 HALF = GROUP // 2
 WORDS = D // 2
 DOC_SPANS = [(0, 512), (512, 704), (704, 768)]
-QUERY_SPANS = [(0, 512)]
+QUERY_SPANS = [(0, 384), (384, 512)]
 Q_GROUPS = NQ // P
 
 
@@ -40,7 +40,7 @@ def tile_efficientspladecentredscores_t_kernel(tc, xq, xd_bytes, xd_scale, wq, w
         ctx.enter_context(tc.manual_schedule())
 
         xq_rows = xq.rearrange("(g p) l d -> g p (l d)", p=P)
-        xd_rows = xd_bytes.rearrange("n l d -> (n l) d").rearrange("(s j p) d -> s p j d", p=P, j=STEP // P)
+        xd_rows = xd_bytes.rearrange("n l d -> (n l) d").rearrange("(s g p j) d -> s p g (j d)", p=P, g=2, j=PACK)
         rows = {}
         xbytes = {}
 
@@ -56,13 +56,14 @@ def tile_efficientspladecentredscores_t_kernel(tc, xq, xd_bytes, xd_scale, wq, w
 
         def load_docs(s):
             t = work.tile([P, STEP // P * D], U8, name="xd_raw", bufs=D_STEPS - 1, align_bytes=64)
-            nc.sync.dma_start(out=t[:].rearrange("p (j d) -> p j d", d=D), in_=xd_rows[s])
+            nc.sync.dma_start(out=t[:].rearrange("p (g c) -> p g c", g=2), in_=xd_rows[s])
             for g in range(2):
                 xbytes[(s, g)] = t[:, g * PACK * D : (g + 1) * PACK * D]
 
         def load_doc_tiles(j0, j1):
             t = keep.tile([P, (j1 - j0) * D], U8, name="xd_first%d" % j0, align_bytes=64)
-            nc.sync.dma_start(out=t[:].rearrange("p (j d) -> p j d", d=D), in_=xd_rows[0][:, j0:j1, :])
+            g = j0 // PACK
+            nc.sync.dma_start(out=t[:], in_=xd_rows[0][:, g, (j0 - PACK * g) * D : (j1 - PACK * g) * D])
             return t[:]
 
         def load_weight(w, name):
@@ -76,8 +77,8 @@ def tile_efficientspladecentredscores_t_kernel(tc, xq, xd_bytes, xd_scale, wq, w
             return t
 
         k_scale = load_vector(xd_scale.rearrange("a c k -> (a c k)"), F32, "k_scale", nc.scalar)
-        wd_raw = load_weight(wd, "wd_raw")
         first_bytes = [load_doc_tiles(0, 2), load_doc_tiles(2, 4)]
+        wd_raw = load_weight(wd, "wd_raw")
         xbytes[(0, 1)] = load_doc_tiles(4, 8)
         for s in range(1, D_STEPS):
             load_docs(s)
@@ -113,16 +114,16 @@ def tile_efficientspladecentredscores_t_kernel(tc, xq, xd_bytes, xd_scale, wq, w
         def plane_tokens(i):
             return {0: 0, 1: GROUP, 2: GROUP + HALF}.get(i, PLANE_TOK)
 
-        def widen(i, g):
+        def widen(i, g, copy=nc.scalar.copy):
             if i >= D_STEPS:
                 return
             t = work.tile([P, PACK * D], BF16, name="xd_wide", bufs=5, align_bytes=64)
-            nc.scalar.copy(out=t[:], in_=xbytes[(i, g)].bitcast(FP8))
+            copy(out=t[:], in_=xbytes[(i, g)].bitcast(FP8))
             set_rows(i, PACK * g, t)
 
-        def widen_first(h):
+        def widen_first(h, copy=nc.scalar.copy):
             t = keep.tile([P, 2 * D], BF16, name="xd_wide_first%d" % h, align_bytes=64)
-            nc.scalar.copy(out=t[:], in_=first_bytes[h].bitcast(FP8))
+            copy(out=t[:], in_=first_bytes[h].bitcast(FP8))
             set_rows(0, 2 * h, t)
 
         def turn(i, g, halves=(0, 1)):
@@ -186,8 +187,8 @@ def tile_efficientspladecentredscores_t_kernel(tc, xq, xd_bytes, xd_scale, wq, w
             )
             packed[i] = t[:]
 
-        def scale_rest(i, g):
-            for bank in (2 * g, 2 * g + 1):
+        def scale_rest(i, g, halves=(0, 1)):
+            for bank in [2 * g + h for h in halves]:
                 k = max(plane_tokens(i) - bank * HALF, 0)
                 if k < HALF:
                     dst = packed[i][:, (bank * HALF + k) * PACK : (bank + 1) * HALF * PACK]
@@ -232,13 +233,13 @@ def tile_efficientspladecentredscores_t_kernel(tc, xq, xd_bytes, xd_scale, wq, w
                 n = GROUP // LQ
                 c = 2 * (i - D_STEPS) + g
                 dst = pooled_q[:, t, c * n : (c + 1) * n]
+                src, axis = logits[(i, g, t)][:].rearrange("p (n l) -> p n l", n=n), AX.X
             else:
                 n = GROUP // LD
                 c = 2 * i + g
                 dst = pooled_d[:, t, c * n : (c + 1) * n]
-            nc.vector.tensor_reduce(
-                out=dst, in_=logits[(i, g, t)][:].rearrange("p (n l) -> p n l", n=n), axis=AX.X, op=ALU.max
-            )
+                src, axis = logits[(i, g, t)][:].rearrange("p (j n c) -> p n j c", j=PACK, n=n), AX.XY
+            nc.vector.tensor_reduce(out=dst, in_=src, axis=axis, op=ALU.max)
 
         def multiply_group(i, g):
             for t in range(PACK):
@@ -275,6 +276,8 @@ def tile_efficientspladecentredscores_t_kernel(tc, xq, xd_bytes, xd_scale, wq, w
         }
 
         def span(which, n, t):
+            if which == "q" and t < 2:
+                return 0, NQ
             return side[which][5][n]
 
         def clamp(which, n, t):
@@ -283,12 +286,12 @@ def tile_efficientspladecentredscores_t_kernel(tc, xq, xd_bytes, xd_scale, wq, w
             nc.scalar.activation(
                 out=pos[:, : c1 - c0], in_=side[which][0][:, t, c0:c1], func=ACT.Relu, bias=b32[:, t : t + 1]
             )
-            positive[t] = pos[:, : c1 - c0]
+            positive[(n, t)] = pos[:, : c1 - c0]
 
         def log1p(which, n, t):
             c0, c1 = span(which, n, t)
             nc.scalar.activation(
-                out=side[which][1][:, t, c0:c1], in_=positive[t], func=ACT.Ln, bias=1.0,
+                out=side[which][1][:, t, c0:c1], in_=positive[(n, t)], func=ACT.Ln, bias=1.0,
                 accum_out=side[which][2][:, n, t : t + 1],
             )
 
@@ -305,19 +308,12 @@ def tile_efficientspladecentredscores_t_kernel(tc, xq, xd_bytes, xd_scale, wq, w
                 scale=gd32[:, t : t + 1], bias=shift_d[:, len(DOC_SPANS) - 1, t : t + 1],
             )
 
-        def query_centre(t):
-            gain, offset = gq32[:, t : t + 1], shift_q[:, len(QUERY_SPANS) - 1, t : t + 1]
-            if t < PACK - 1:
-                nc.gpsimd.tensor_scalar(
-                    out=cq_view[:, :, t, :], in0=r_q[:, t, :].rearrange("p (g n) -> p g n", n=P),
-                    scalar1=gain, scalar2=offset, op0=ALU.mult, op1=ALU.add,
-                )
-                return
-            for g in range(Q_GROUPS):
-                nc.scalar.activation(
-                    out=cq_view[:, g, t, :], in_=r_q[:, t, g * P : (g + 1) * P], func=ACT.Identity,
-                    scale=gain, bias=offset,
-                )
+        def query_centre(engine, t, g0=0, g1=Q_GROUPS):
+            engine.tensor_scalar(
+                out=cq_view[:, g0:g1, t, :], in0=r_q[:, t, g0 * P : g1 * P].rearrange("p (g n) -> p g n", n=P),
+                scalar1=gq32[:, t : t + 1], scalar2=shift_q[:, len(QUERY_SPANS) - 1, t : t + 1],
+                op0=ALU.mult, op1=ALU.add,
+            )
 
         def each_t(job, *args):
             for t in range(PACK):
@@ -338,32 +334,32 @@ def tile_efficientspladecentredscores_t_kernel(tc, xq, xd_bytes, xd_scale, wq, w
             if i == last_doc and half == 1:
                 each_t(shift, "d", 1)
 
-        widen_first(0)
         wd_packed = keep.tile([P, V * PACK], BF16, name="wd_packed", align_bytes=64)
-        dst, src = weight_views(wd_packed[:], wd_raw)
-        nc.vector.tensor_copy(out=dst, in_=src)
-        turn(0, 0, (0,))
-        widen_first(1)
-        turn(0, 0, (1,))
-        weights["d"] = quantize(wd_packed[:], V, "wd", 1)
-        widen(0, 1)
-        turn(0, 1)
-        widen(1, 0)
-        widen(1, 1)
         first = new_packed()
         packed[0] = first[:]
-        for g in range(2):
-            packed[(0, g)] = first[:, g * GROUP * PACK : (g + 1) * GROUP * PACK]
-        scale_rest(0, 0)
-        quantize_group(0, 0)
-        turn(1, 0)
-        multiply_group(0, 0)
-        empty(1, 0)
-        scale_rest(0, 1)
-        turn(1, 1)
-        widen(2, 0)
-        widen(2, 1)
-        quantize_group(0, 1)
+        packed[(0, 0)] = first[:, : GROUP * PACK]
+        packed[(0, 1)] = first[:, GROUP * PACK :]
+        widen_first(0)
+        gpsimd_copy(*weight_views(wd_packed[:], wd_raw))
+        turn(0,0,(0,))
+        widen_first(1)
+        turn(0,0,(1,))
+        widen(0,1)
+        turn(0,1)
+        widen(1,0)
+        widen(1,1)
+        scale_rest(0,0)
+        turn(1,0)
+        scale_rest(0,1,(0,))
+        weights["d"] = quantize(wd_packed[:], V, "wd", 1)
+        quantize_group(0,0)
+        multiply_group(0,0)
+        empty(1,0)
+        scale_rest(0,1,(1,))
+        turn(1,1)
+        widen(2,0)
+        widen(2,1)
+        quantize_group(0,1)
         interleave(1)
         turn(2, 0)
         pool_group(0, 0)
@@ -403,7 +399,9 @@ def tile_efficientspladecentredscores_t_kernel(tc, xq, xd_bytes, xd_scale, wq, w
 
         weights["q"] = quantize(wq_packed[:, : V * PACK], V, "wq", 1)
         q_groups = [(i, g) for i in range(D_STEPS, STEPS) for g in range(2)]
-        order = [(i, g, t) for t in range(PACK) for i, g in q_groups]
+        order = [(i, g, t) for t in (0, 1) for i, g in q_groups]
+        order += [(i, g, t) for t in (2, 3) for i, g in q_groups[:-1]]
+        order += [q_groups[-1] + (t,) for t in (2, 3)]
         for i, g in q_groups:
             quantize_group(i, g)
             multiply(i, g, 0)
@@ -413,10 +411,24 @@ def tile_efficientspladecentredscores_t_kernel(tc, xq, xd_bytes, xd_scale, wq, w
             pool_max(i, g, t)
             if n + 4 < len(order):
                 multiply(*order[n + 4])
-            if n % 4 == 3:
+            if n in (3, 7):
                 for job in (clamp, log1p, shift):
-                    job("q", 0, t)
-                query_centre(t)
+                    job("q", 1, t)
+                query_centre(nc.gpsimd, t)
+            if n == 10:
+                for job in (clamp, log1p, shift):
+                    job("q", 0, 2)
+            if n == 13:
+                clamp("q", 0, 3)
+            if n == 14:
+                clamp("q", 1, 2)
+                log1p("q", 0, 3)
+                log1p("q", 1, 2)
+        clamp("q", 1, 3)
+        shift("q", 1, 2)
+        shift("q", 0, 3)
+        log1p("q", 1, 3)
+        shift("q", 1, 3)
         cd_quant = [
             quantize(cd_packed[:, c0 * PACK : c1 * PACK], c1 - c0, "cd%d" % c0, 1) for c0, c1 in ((0, GROUP), (GROUP, ND))
         ]
@@ -461,6 +473,9 @@ def tile_efficientspladecentredscores_t_kernel(tc, xq, xd_bytes, xd_scale, wq, w
                 nc.sync.dma_start(out=rows_out, in_=res[:])
 
         on_scalar, on_vector = nc.scalar.copy, nc.vector.tensor_copy
+        query_centre(nc.vector, 2)
+        query_centre(nc.vector, 3, 0, 1)
+        query_centre(nc.vector, 3, 1, Q_GROUPS)
         pack_queries(0)
         pack_queries(1)
         scores(0)

@@ -23,7 +23,7 @@ STEP = 1024
 Q_STEPS = NQ * LQ // STEP
 D_STEPS = ND * LD // STEP
 STEPS = Q_STEPS + D_STEPS
-PLANE_TOK = 832
+PLANE_TOK = 848
 HALF = GROUP // 2
 WORDS = D // 2
 DOC_SPANS = [(0, 512), (512, 704), (704, 768)]
@@ -91,8 +91,17 @@ def tile_efficientspladecentredscores_t_kernel(tc, xq, xd_bytes, xd_scale, wq, w
 
         ident = keep.tile([P, P], F32, name="ident")
         make_identity(nc, ident[:])
+        zeros = keep.tile([P, GROUP], BF16, name="zeros", align_bytes=64)
+        nc.vector.memset(zeros[:], 0.0)
         warm = keep.tile([P, 1], F32, name="warm")
-        nc.scalar.activation(out=warm[:], in_=ident[:, 0:1], func=ACT.Ln, bias=1.0)
+        nc.scalar.activation(out=warm[:], in_=zeros[:, 0:1], func=ACT.Ln, bias=1.0)
+
+        def keep_clock(count, moving=zeros[:]):
+            idle = psum.tile([P, GROUP], F32, name="acc", bufs=4)
+            for n in range(count):
+                nc.tensor.matmul(idle[:], lhsT=zeros[:, :P], rhs=moving, start=True, stop=True)
+
+        keep_clock(10)
 
         pooled_q = keep.tile([P, PACK, NQ], F32, name="pooled_q")
         pooled_d = keep.tile([P, PACK, ND], F32, name="pooled_d")
@@ -344,12 +353,15 @@ def tile_efficientspladecentredscores_t_kernel(tc, xq, xd_bytes, xd_scale, wq, w
         turn(0,0,(0,))
         widen_first(1)
         turn(0,0,(1,))
+        keep_clock(2)
         widen(0,1)
-        turn(0,1)
+        turn(0,1,(0,))
+        turn(0,1,(1,))
         widen(1,0)
         widen(1,1)
         scale_rest(0,0)
-        turn(1,0)
+        turn(1,0,(0,))
+        turn(1,0,(1,))
         scale_rest(0,1,(0,))
         weights["d"] = quantize(wd_packed[:], V, "wd", 1)
         quantize_group(0,0)
@@ -411,6 +423,8 @@ def tile_efficientspladecentredscores_t_kernel(tc, xq, xd_bytes, xd_scale, wq, w
             pool_max(i, g, t)
             if n + 4 < len(order):
                 multiply(*order[n + 4])
+            else:
+                keep_clock(1)
             if n in (3, 7):
                 for job in (clamp, log1p, shift):
                     job("q", 1, t)
@@ -474,6 +488,7 @@ def tile_efficientspladecentredscores_t_kernel(tc, xq, xd_bytes, xd_scale, wq, w
 
         on_scalar, on_vector = nc.scalar.copy, nc.vector.tensor_copy
         query_centre(nc.vector, 2)
+        keep_clock(2, cq_view[:, :, 2, :])
         query_centre(nc.vector, 3, 0, 1)
         query_centre(nc.vector, 3, 1, Q_GROUPS)
         pack_queries(0)

@@ -23,7 +23,7 @@ STEP = 1024
 Q_STEPS = NQ * LQ // STEP
 D_STEPS = ND * LD // STEP
 STEPS = Q_STEPS + D_STEPS
-PLANE_TOK = 848
+PLANE_TOK = 864
 HALF = GROUP // 2
 WORDS = D // 2
 DOC_SPANS = [(0, 512), (512, 704), (704, 768)]

from contextlib import ExitStack

import concourse.mybir as mybir
from concourse.masks import make_identity

NQ, LQ, ND, LD, D, V = 512, 4, 768, 16, 512, 512
FLOPS = 2 * (NQ * LQ + ND * LD) * D * V + 2 * NQ * ND * V

F32 = mybir.dt.float32
BF16 = mybir.dt.bfloat16
U32 = mybir.dt.uint32
U8 = mybir.dt.uint8
FP8 = mybir.dt.float8_e4m3fn
FP8X4 = mybir.dt.float8_e4m3fn_x4
ACT = mybir.ActivationFunctionType
ALU = mybir.AluOpType
AX = mybir.AxisListType

P = 128
PACK = 4
GROUP = 512
STEP = 1024
Q_STEPS = NQ * LQ // STEP
D_STEPS = ND * LD // STEP
STEPS = Q_STEPS + D_STEPS
PLANE_TOK = 864
HALF = GROUP // 2
WORDS = D // 2
DOC_SPANS = [(0, 512), (512, 704), (704, 768)]
QUERY_SPANS = [(0, 384), (384, 512)]
Q_GROUPS = NQ // P


def tile_efficientspladecentredscores_t_kernel(tc, xq, xd_bytes, xd_scale, wq, wd, b, gq, gd, out):
    nc = tc.nc
    with ExitStack() as ctx:
        keep = ctx.enter_context(tc.tile_pool(name="keep", bufs=1))
        work = ctx.enter_context(tc.tile_pool(name="work", bufs=1))
        psum = ctx.enter_context(tc.psum_pool(name="psum", bufs=1))
        ctx.enter_context(tc.manual_schedule())

        xq_rows = xq.rearrange("(g p) l d -> g p (l d)", p=P)
        xd_rows = xd_bytes.rearrange("n l d -> (n l) d").rearrange("(s g p j) d -> s p g (j d)", p=P, g=2, j=PACK)
        rows = {}
        xbytes = {}

        def set_rows(i, j0, t):
            words = t[:].bitcast(F32)
            for j in range(words.shape[1] // WORDS):
                rows[(i, j0 + j)] = words[:, j * WORDS : (j + 1) * WORDS]

        def load_queries(g):
            t = work.tile([P, LQ * D], BF16, name="xq_raw", bufs=4, align_bytes=64)
            nc.sync.dma_start(out=t[:], in_=xq_rows[g])
            set_rows(D_STEPS + g // 2, PACK * (g % 2), t)

        def load_docs(s):
            t = work.tile([P, STEP // P * D], U8, name="xd_raw", bufs=D_STEPS - 1, align_bytes=64)
            nc.sync.dma_start(out=t[:].rearrange("p (g c) -> p g c", g=2), in_=xd_rows[s])
            for g in range(2):
                xbytes[(s, g)] = t[:, g * PACK * D : (g + 1) * PACK * D]

        def load_doc_tiles(j0, j1):
            t = keep.tile([P, (j1 - j0) * D], U8, name="xd_first%d" % j0, align_bytes=64)
            g = j0 // PACK
            nc.sync.dma_start(out=t[:], in_=xd_rows[0][:, g, (j0 - PACK * g) * D : (j1 - PACK * g) * D])
            return t[:]

        def load_weight(w, name):
            t = keep.tile([P, PACK, V], BF16, name=name, align_bytes=64)
            nc.sync.dma_start(out=t[:], in_=w.rearrange("(p j) c -> p j c", j=PACK))
            return t

        def load_vector(vec, dtype, name, queue=nc.sync):
            t = keep.tile([P, PACK], dtype, name=name)
            queue.dma_start(out=t[:], in_=vec.rearrange("(p t) -> p t", t=PACK))
            return t

        k_scale = load_vector(xd_scale.rearrange("a c k -> (a c k)"), F32, "k_scale", nc.scalar)
        first_bytes = [load_doc_tiles(0, 2), load_doc_tiles(2, 4)]
        wd_raw = load_weight(wd, "wd_raw")
        xbytes[(0, 1)] = load_doc_tiles(4, 8)
        for s in range(1, D_STEPS):
            load_docs(s)
        b_raw = load_vector(b, BF16, "b_raw")
        gq_raw = load_vector(gq, BF16, "gq_raw")
        gd_raw = load_vector(gd, BF16, "gd_raw")
        wq_raw = load_weight(wq, "wq_raw")
        for g in range(Q_GROUPS):
            load_queries(g)

        ident = keep.tile([P, P], F32, name="ident")
        make_identity(nc, ident[:])
        zeros = keep.tile([P, GROUP], BF16, name="zeros", align_bytes=64)
        nc.vector.memset(zeros[:], 0.0)
        warm = keep.tile([P, 1], F32, name="warm")
        nc.scalar.activation(out=warm[:], in_=zeros[:, 0:1], func=ACT.Ln, bias=1.0)

        def keep_clock(count, moving=zeros[:]):
            idle = psum.tile([P, GROUP], F32, name="acc", bufs=4)
            for n in range(count):
                nc.tensor.matmul(idle[:], lhsT=zeros[:, :P], rhs=moving, start=True, stop=True)

        keep_clock(10)

        pooled_q = keep.tile([P, PACK, NQ], F32, name="pooled_q")
        pooled_d = keep.tile([P, PACK, ND], F32, name="pooled_d")
        r_q, r_d = pooled_q, pooled_d

        def quantize(src, width, name, bufs):
            codes = work.tile([P, width], U32, name=name + "_codes", bufs=bufs, align_bytes=64)
            scales = work.tile([P, width], U8, name=name + "_scales", bufs=bufs, align_bytes=64)
            nc.vector.quantize_mx(out=codes[:].bitcast(FP8X4), scales=scales[:], in_=src)
            return codes, scales

        banks = {}
        planes = {}
        packed = {}
        quant = {}
        logits = {}
        weights = {}

        def plane_tokens(i):
            return {0: 0, 1: GROUP, 2: GROUP + HALF}.get(i, PLANE_TOK)

        def widen(i, g, copy=nc.scalar.copy):
            if i >= D_STEPS:
                return
            t = work.tile([P, PACK * D], BF16, name="xd_wide", bufs=5, align_bytes=64)
            copy(out=t[:], in_=xbytes[(i, g)].bitcast(FP8))
            set_rows(i, PACK * g, t)

        def widen_first(h, copy=nc.scalar.copy):
            t = keep.tile([P, 2 * D], BF16, name="xd_wide_first%d" % h, align_bytes=64)
            copy(out=t[:], in_=first_bytes[h].bitcast(FP8))
            set_rows(0, 2 * h, t)

        def turn(i, g, halves=(0, 1)):
            for h in halves:
                if i >= D_STEPS:
                    slots = [(2 * h + l, u) for l in range(2) for u in range(2)]
                elif plane_tokens(i) >= (g + 1) * GROUP:
                    slots = [(j, h) for j in range(4)]
                else:
                    slots = [(2 * h + j, u) for u in range(2) for j in range(2)]
                bank = psum.tile([P, 512], F32, name="turn%d" % (2 * g + h))
                for n, (j, u) in enumerate(slots):
                    nc.tensor.transpose(
                        bank[:, n * P : (n + 1) * P], rows[(i, PACK * g + j)][:, u::2], ident[:]
                    )
                banks[(i, 2 * g + h)] = bank

        def empty(i, g):
            if i >= D_STEPS:
                if (i, g) == (STEPS - 1, 1):
                    t = work.tile([P, GROUP * PACK], BF16, name="late_packed", bufs=1, align_bytes=64)
                else:
                    t = work.tile([P, GROUP * PACK], BF16, name="q_packed", bufs=3, align_bytes=64)
                dst = t[:].bitcast(F32).rearrange("p (q h s) -> p q h s", h=2, s=4)
                for h in range(2):
                    nc.scalar.copy(out=dst[:, :, h, :], in_=banks[(i, 2 * g + h)][:].rearrange("p (s q) -> p q s", s=4))
                packed[(i, g)] = t[:]
                return
            n = plane_tokens(i)
            parts = []
            if n >= (g + 1) * GROUP:
                pl = work.tile([P, PACK, PLANE_TOK], BF16, name="planes", bufs=2, align_bytes=64)
                planes[i] = pl
                parts = [(banks[(i, u)][:], u, 0, GROUP) for u in range(2)]
            else:
                for bank in (2 * g, 2 * g + 1):
                    k = min(n - bank * HALF, HALF)
                    if k > 0:
                        for u in range(2):
                            parts.append((banks[(i, bank)][:, u * HALF : u * HALF + k], u, bank * HALF, bank * HALF + k))
            for src, u, c0, c1 in parts:
                pairs = src.bitcast(BF16).rearrange("p (n e) -> p n e", e=2)
                for e in range(2):
                    t = 2 * u + e
                    nc.scalar.activation(
                        out=planes[i][:, t, c0:c1], in_=pairs[:, :, e], func=ACT.Copy, scale=k_scale[:, t : t + 1]
                    )

        def gpsimd_copy(dst, src):
            nc.gpsimd.tensor_scalar(out=dst, in0=src, scalar1=1.0, scalar2=0.0, op0=ALU.mult, op1=ALU.add)

        def new_packed():
            t = work.tile([P, STEP * PACK], BF16, name="d_packed", bufs=1, align_bytes=64)
            return t

        def interleave(i):
            t = new_packed()
            n = plane_tokens(i)
            gpsimd_copy(
                t[:, : n * PACK].rearrange("p (n t) -> p n t", t=PACK), planes[i][:, :, :n].rearrange("p t n -> p n t")
            )
            packed[i] = t[:]

        def scale_rest(i, g, halves=(0, 1)):
            for bank in [2 * g + h for h in halves]:
                k = max(plane_tokens(i) - bank * HALF, 0)
                if k < HALF:
                    dst = packed[i][:, (bank * HALF + k) * PACK : (bank + 1) * HALF * PACK]
                    nc.vector.tensor_tensor(
                        out=dst.rearrange("p (n u e) -> p n u e", u=2, e=2),
                        in0=banks[(i, bank)][:].bitcast(BF16).rearrange("p (u n e) -> p n u e", u=2, e=2)[:, k:, :, :],
                        in1=k_scale[:].rearrange("p (o u e) -> p o u e", o=1, u=2).to_broadcast([P, HALF - k, 2, 2]),
                        op=ALU.mult,
                    )

        def quantize_group(i, g):
            quant[(i, g)] = quantize(packed[(i, g)], GROUP, "x", 4)

        def quantize_step(i):
            codes, scales = quantize(packed[i], STEP, "d", 3)
            for g in range(2):
                quant[(i, g)] = (codes[:, g * GROUP : (g + 1) * GROUP], scales[:, g * GROUP : (g + 1) * GROUP])

        def weight_views(dst, raw):
            return (
                dst.rearrange("p (t m j) -> p t m j", t=PACK, j=PACK),
                raw[:].rearrange("p j (m t) -> p t m j", t=PACK),
            )

        def multiply(i, g, t):
            w_codes, w_scales = weights["q" if i >= D_STEPS else "d"]
            codes, scales = quant[(i, g)]
            acc = psum.tile([P, GROUP], F32, name="acc", bufs=4)
            nc.tensor.matmul_mx(
                out=acc[:],
                lhsT=w_codes[:, t * P : (t + 1) * P].bitcast(FP8X4),
                lhsT_scale=w_scales[:, t * P : (t + 1) * P],
                rhs=codes[:].bitcast(FP8X4),
                rhs_scale=scales[:],
                start=True,
                stop=True,
            )
            logits[(i, g, t)] = acc

        def pool_max(i, g, t):
            if i >= D_STEPS:
                n = GROUP // LQ
                c = 2 * (i - D_STEPS) + g
                dst = pooled_q[:, t, c * n : (c + 1) * n]
                src, axis = logits[(i, g, t)][:].rearrange("p (n l) -> p n l", n=n), AX.X
            else:
                n = GROUP // LD
                c = 2 * i + g
                dst = pooled_d[:, t, c * n : (c + 1) * n]
                src, axis = logits[(i, g, t)][:].rearrange("p (j n c) -> p n j c", j=PACK, n=n), AX.XY
            nc.vector.tensor_reduce(out=dst, in_=src, axis=axis, op=ALU.max)

        def multiply_group(i, g):
            for t in range(PACK):
                multiply(i, g, t)

        def pool_group(i, g):
            for t in range(PACK):
                pool_max(i, g, t)

        b32 = keep.tile([P, PACK], F32, name="b32")
        gq32 = keep.tile([P, PACK], F32, name="gq32")
        gd32 = keep.tile([P, PACK], F32, name="gd32")
        gq_mean = keep.tile([P, PACK], F32, name="gq_mean")
        gd_mean = keep.tile([P, PACK], F32, name="gd_mean")
        sum_q = keep.tile([P, len(QUERY_SPANS), PACK], F32, name="sum_q")
        shift_q = keep.tile([P, len(QUERY_SPANS), PACK], F32, name="shift_q")
        sum_d = keep.tile([P, len(DOC_SPANS), PACK], F32, name="sum_d")
        shift_d = keep.tile([P, len(DOC_SPANS), PACK], F32, name="shift_d")
        cd_planes = keep.tile([P, PACK, ND], BF16, name="cd_planes", align_bytes=64)
        cq_planes = keep.tile([P, NQ * PACK], BF16, name="cq_planes", align_bytes=64)
        cq_view = cq_planes[:].rearrange("p (g t n) -> p g t n", t=PACK, n=P)

        def constants():
            nc.scalar.activation(out=b32[:], in_=b_raw[:], func=ACT.Copy)
            nc.scalar.activation(out=gq32[:], in_=gq_raw[:], func=ACT.Copy)
            nc.scalar.activation(out=gd32[:], in_=gd_raw[:], func=ACT.Copy)
            nc.scalar.activation(out=gq_mean[:], in_=gq_raw[:], func=ACT.Copy, scale=-1.0 / NQ)
            nc.scalar.activation(out=gd_mean[:], in_=gd_raw[:], func=ACT.Copy, scale=-1.0 / ND)

        positive = {}
        side = {
            "q": (pooled_q, r_q, sum_q, shift_q, gq_mean, QUERY_SPANS),
            "d": (pooled_d, r_d, sum_d, shift_d, gd_mean, DOC_SPANS),
        }

        def span(which, n, t):
            if which == "q" and t < 2:
                return 0, NQ
            return side[which][5][n]

        def clamp(which, n, t):
            c0, c1 = span(which, n, t)
            pos = work.tile([P, GROUP], F32, name="pos", bufs=4)
            nc.scalar.activation(
                out=pos[:, : c1 - c0], in_=side[which][0][:, t, c0:c1], func=ACT.Relu, bias=b32[:, t : t + 1]
            )
            positive[(n, t)] = pos[:, : c1 - c0]

        def log1p(which, n, t):
            c0, c1 = span(which, n, t)
            nc.scalar.activation(
                out=side[which][1][:, t, c0:c1], in_=positive[(n, t)], func=ACT.Ln, bias=1.0,
                accum_out=side[which][2][:, n, t : t + 1],
            )

        def shift(which, n, t):
            sums, shifts, gain = side[which][2:5]
            nc.scalar.activation(
                out=shifts[:, n, t : t + 1], in_=sums[:, n, t : t + 1], func=ACT.Identity,
                scale=gain[:, t : t + 1], bias=shifts[:, n - 1, t : t + 1] if span(which, n, t)[0] else 0.0,
            )

        def doc_centre(t):
            nc.scalar.activation(
                out=cd_planes[:, t, :], in_=r_d[:, t, :], func=ACT.Identity,
                scale=gd32[:, t : t + 1], bias=shift_d[:, len(DOC_SPANS) - 1, t : t + 1],
            )

        def query_centre(engine, t, g0=0, g1=Q_GROUPS):
            engine.tensor_scalar(
                out=cq_view[:, g0:g1, t, :], in0=r_q[:, t, g0 * P : g1 * P].rearrange("p (g n) -> p g n", n=P),
                scalar1=gq32[:, t : t + 1], scalar2=shift_q[:, len(QUERY_SPANS) - 1, t : t + 1],
                op0=ALU.mult, op1=ALU.add,
            )

        def each_t(job, *args):
            for t in range(PACK):
                job(*args, t)

        last_doc = D_STEPS - 1

        def extra(i, half):
            if i == last_doc - 3 and half == 1:
                constants()
            if i in (last_doc - 2, last_doc - 1):
                for t in range(2):
                    (clamp, log1p)[half]("d", 0, 2 * (i - last_doc + 2) + t)
            if i == last_doc and half == 0:
                each_t(clamp, "d", 1)
                each_t(shift, "d", 0)
                each_t(log1p, "d", 1)
            if i == last_doc and half == 1:
                each_t(shift, "d", 1)

        wd_packed = keep.tile([P, V * PACK], BF16, name="wd_packed", align_bytes=64)
        first = new_packed()
        packed[0] = first[:]
        packed[(0, 0)] = first[:, : GROUP * PACK]
        packed[(0, 1)] = first[:, GROUP * PACK :]
        widen_first(0)
        gpsimd_copy(*weight_views(wd_packed[:], wd_raw))
        turn(0,0,(0,))
        widen_first(1)
        turn(0,0,(1,))
        keep_clock(2)
        widen(0,1)
        turn(0,1,(0,))
        turn(0,1,(1,))
        widen(1,0)
        widen(1,1)
        scale_rest(0,0)
        turn(1,0,(0,))
        turn(1,0,(1,))
        scale_rest(0,1,(0,))
        weights["d"] = quantize(wd_packed[:], V, "wd", 1)
        quantize_group(0,0)
        multiply_group(0,0)
        empty(1,0)
        scale_rest(0,1,(1,))
        turn(1,1)
        widen(2,0)
        widen(2,1)
        quantize_group(0,1)
        interleave(1)
        turn(2, 0)
        pool_group(0, 0)
        multiply_group(0, 1)
        empty(2, 0)
        widen(3, 0)
        scale_rest(1, 1)
        turn(2, 1)
        empty(2, 1)
        widen(3, 1)

        for i in range(1, D_STEPS):
            quantize_step(i)
            if i < last_doc:
                interleave(i + 1)
            else:
                wq_packed = new_packed()
                gpsimd_copy(*weight_views(wq_packed[:, : V * PACK], wq_raw))
            turn(i + 2, 0)
            pool_group(i - 1, 1)
            multiply_group(i, 0)
            empty(i + 2, 0)
            extra(i, 0)
            widen(i + 3, 0)
            if i < last_doc:
                scale_rest(i + 1, 1)
            turn(i + 2, 1)
            pool_group(i, 0)
            multiply_group(i, 1)
            empty(i + 2, 1)
            extra(i, 1)
            widen(i + 3, 1)
        pool_group(last_doc, 1)
        for job in (clamp, log1p, shift):
            each_t(job, "d", len(DOC_SPANS) - 1)
        each_t(doc_centre)

        weights["q"] = quantize(wq_packed[:, : V * PACK], V, "wq", 1)
        q_groups = [(i, g) for i in range(D_STEPS, STEPS) for g in range(2)]
        order = [(i, g, t) for t in (0, 1) for i, g in q_groups]
        order += [(i, g, t) for t in (2, 3) for i, g in q_groups[:-1]]
        order += [q_groups[-1] + (t,) for t in (2, 3)]
        for i, g in q_groups:
            quantize_group(i, g)
            multiply(i, g, 0)
        cd_packed = work.tile([P, ND * PACK], BF16, name="late_packed", bufs=1, align_bytes=64)
        gpsimd_copy(cd_packed[:].rearrange("p (n t) -> p n t", t=PACK), cd_planes[:].rearrange("p t n -> p n t"))
        for n, (i, g, t) in enumerate(order):
            pool_max(i, g, t)
            if n + 4 < len(order):
                multiply(*order[n + 4])
            else:
                keep_clock(1)
            if n in (3, 7):
                for job in (clamp, log1p, shift):
                    job("q", 1, t)
                query_centre(nc.gpsimd, t)
            if n == 10:
                for job in (clamp, log1p, shift):
                    job("q", 0, 2)
            if n == 13:
                clamp("q", 0, 3)
            if n == 14:
                clamp("q", 1, 2)
                log1p("q", 0, 3)
                log1p("q", 1, 2)
        clamp("q", 1, 3)
        shift("q", 1, 2)
        shift("q", 0, 3)
        log1p("q", 1, 3)
        shift("q", 1, 3)
        cd_quant = [
            quantize(cd_packed[:, c0 * PACK : c1 * PACK], c1 - c0, "cd%d" % c0, 1) for c0, c1 in ((0, GROUP), (GROUP, ND))
        ]

        cq_packed = {}
        score_banks = {}

        def pack_queries(g):
            t = work.tile([P, P * PACK], BF16, name="cq_packed", bufs=Q_GROUPS, align_bytes=64)
            nc.vector.tensor_copy(
                out=t[:].rearrange("p (n t) -> p n t", t=PACK), in_=cq_view[:, g, :, :].rearrange("p t n -> p n t")
            )
            cq_packed[g] = t

        def scores(g):
            codes, scales = quantize(cq_packed[g][:], P, "cq", Q_GROUPS)
            wide = psum.tile([P, GROUP], F32, name="acc", bufs=4)
            narrow = psum.tile([P, GROUP], F32, name="turn%d" % g)
            score_banks[g] = (wide[:], narrow[:, : ND - GROUP])
            for part in (1, 0):
                d_codes, d_scales = cd_quant[part]
                nc.tensor.matmul_mx(
                    out=score_banks[g][part],
                    lhsT=codes[:].bitcast(FP8X4),
                    lhsT_scale=scales[:],
                    rhs=d_codes[:].bitcast(FP8X4),
                    rhs_scale=d_scales[:],
                    start=True,
                    stop=True,
                )

        def store(g, copies):
            res = work.tile([P, ND], F32, name="res", bufs=Q_GROUPS)
            rows_out = out[g * P : (g + 1) * P, :]
            copies[1](out=res[:, GROUP:], in_=score_banks[g][1])
            if g == 0:
                nc.sync.dma_start(out=rows_out[:, GROUP:], in_=res[:, GROUP:])
            copies[0](out=res[:, :GROUP], in_=score_banks[g][0])
            if g == 0:
                nc.sync.dma_start(out=rows_out[:, :GROUP], in_=res[:, :GROUP])
            else:
                nc.sync.dma_start(out=rows_out, in_=res[:])

        on_scalar, on_vector = nc.scalar.copy, nc.vector.tensor_copy
        query_centre(nc.vector, 2)
        keep_clock(2, cq_view[:, :, 2, :])
        query_centre(nc.vector, 3, 0, 1)
        query_centre(nc.vector, 3, 1, Q_GROUPS)
        pack_queries(0)
        pack_queries(1)
        scores(0)
        pack_queries(2)
        scores(1)
        pack_queries(3)
        scores(2)
        scores(3)
        store(0, (on_scalar, on_scalar))
        store(1, (on_scalar, on_vector))
        store(2, (on_scalar, on_vector))
        store(3, (on_vector, on_scalar))
